import numpy as np
import ml_dtypes


def mxq(x, axis, fmt="e4m3"):
    dtype, down = {"e4m3": (ml_dtypes.float8_e4m3fn, 7), "e5m2": (ml_dtypes.float8_e5m2, 14)}[fmt]
    v = np.moveaxis(np.asarray(x, np.float32).astype(ml_dtypes.bfloat16).astype(np.float64), axis, -1)
    blocks = v.reshape(v.shape[:-1] + (-1, 32))
    amax = np.abs(blocks).max(-1, keepdims=True)
    byte = np.maximum(np.where(amax > 0, np.frexp(amax)[1] - 1 + 127, 0) - down, 1)
    scale = np.exp2(byte - 127.0)
    codes = (blocks / scale).astype(np.float32).astype(dtype).astype(np.float64)
    return np.moveaxis((codes * scale).reshape(v.shape), -1, axis)


WIDE = False


def mx_kscale(k):
    if not WIDE:
        return np.ones(k)
    levels = np.array([10, -10, 5, -5, 0])
    if k % 512:
        return np.exp2(np.random.permutation(np.resize(levels, k // 32))).repeat(32)
    a = np.empty((k // 512, 16))
    for p in range(k // 512):
        a[p, :8] = np.random.permutation(np.resize(levels, 8))
        for g in range(8):
            far = levels[np.abs(levels - a[p, g]) >= 10]
            a[p, g + 8] = far[np.random.randint(len(far))]
    return np.exp2(a.ravel()).repeat(32)


def f64(x):
    return np.asarray(x).astype(np.float64)


def striped(idx):
    return np.tile(idx.reshape(-1, 16).T, (8, 1)).astype(np.uint16)


def unstriped(offs):
    return offs[:16].T.reshape(-1).astype(np.int64)


def pack_weight(w):
    k, n = w.shape
    w = f64(np.asarray(w, np.float32).astype(ml_dtypes.bfloat16)).reshape(k // 32, 32, n)
    amax = np.abs(w).max(1)
    byte = np.clip(np.where(amax > 0, np.frexp(amax)[1] - 1 + 127 - 7, 1), 1, 254)
    scaled = (w * np.exp2(127.0 - byte)[:, None, :]).reshape(k, n).astype(np.float32)
    words = np.ascontiguousarray(scaled.reshape(k // 512, 128, 4, n).transpose(0, 1, 3, 2)).astype(ml_dtypes.float8_e4m3fn).view(np.uint8)
    return words, np.ascontiguousarray(byte.astype(np.uint8).reshape(k // 512, 16, n))


def unpack_weight(words, scales):
    g, p, n, _ = words.shape
    vals = np.ascontiguousarray(words).view(ml_dtypes.float8_e4m3fn).astype(np.float64) * np.repeat(np.exp2(scales.astype(np.float64) - 127.0), 8, axis=1)[..., None]
    return vals.transpose(0, 1, 3, 2).reshape(g * 512, n)


E2M1 = np.array([0.0, 0.5, 1.0, 1.5, 2.0, 3.0, 4.0, 6.0, -0.0, -0.5, -1.0, -1.5, -2.0, -3.0, -4.0, -6.0])


def pack_fp4(w):
    k, n = w.shape
    w = f64(np.asarray(w, np.float32).astype(ml_dtypes.bfloat16)).reshape(k // 32, 32, n)
    amax = np.abs(w).max(1)
    mant, ex = np.frexp(amax / 6.0)
    byte = np.clip(np.where(amax > 0, np.where(mant > 0.5, ex, ex - 1) + 127, 1), 1, 254)
    scaled = (w * np.exp2(127.0 - byte)[:, None, :]).reshape(k, n).astype(np.float32)
    c = np.ascontiguousarray(scaled.reshape(k // 512, 128, 4, n).transpose(0, 1, 3, 2)).astype(ml_dtypes.float4_e2m1fn).view(np.uint8) & 0xF
    words = (c[..., 0::2] | (c[..., 1::2] << 4)).reshape(k // 512, 128, 2 * n)
    return np.ascontiguousarray(words), np.ascontiguousarray(byte.astype(np.uint8).reshape(k // 512, 16, n))


def unpack_fp4(words, scales):
    g, _, n = scales.shape
    words = np.ascontiguousarray(words).reshape(g, 128, n, 2)
    nib = np.empty((g, 128, n, 4), np.uint8)
    nib[..., 0::2] = words & 0xF
    nib[..., 1::2] = words >> 4
    vals = E2M1[nib] * np.repeat(np.exp2(scales.astype(np.float64) - 127.0), 8, axis=1)[..., None]
    return vals.transpose(0, 1, 3, 2).reshape(g * 512, n)


K, T, S, D, N, H, V, U = 512, 2048, 1024, 4, 256, 512, 256, 512


def setup_inputs():
    n = np.random.standard_normal
    s = mx_kscale(K)[:, None]
    u = mx_kscale(H)
    packed_xT = pack_weight(n((K, T)) * s)
    packed_w1 = pack_fp4(n((K, H)) / np.sqrt(K) / s)
    packed_w2 = pack_fp4(n((K, H)) / np.sqrt(K) / s)
    packed_w3 = pack_fp4(n((H, N)) / np.sqrt(H) / u[:, None])
    return {
        "x_words": packed_xT[0],
        "x_scales": packed_xT[1],
        "w1_words": packed_w1[0],
        "w1_scales": packed_w1[1],
        "w2_words": packed_w2[0],
        "w2_scales": packed_w2[1],
        "ref": (0.6 * n((H, S))).astype(np.float32),
        "unit": (np.random.uniform(0.6, 1.4, (H, 1)) * u[:, None]).astype(np.float32),
        "w3_words": packed_w3[0],
        "w3_scales": packed_w3[1],
        "offs": striped(np.random.permutation(T)[:S]),
        "nl": striped(np.random.permutation(S)),
        "lib": striped(np.random.permutation(np.concatenate([np.arange(V), np.random.randint(0, V, U - V)]))),
    }


def reference(x_words, x_scales, w1_words, w1_scales, w2_words, w2_scales, ref, unit, w3_words, w3_scales, offs, nl, lib):
    xq = unpack_weight(x_words, x_scales)[:, unstriped(offs)]
    it = unpack_fp4(w1_words, w1_scales).T @ xq
    inten = np.log(np.exp(it) + 1.0)
    in_ = inten[:, unstriped(nl)]
    mz = unpack_fp4(w2_words, w2_scales).T @ xq
    mzz = np.tanh(mz)
    mn = mzz[:, unstriped(nl)]
    loss = mzz - mn
    mtch = np.exp(-1.5 * ((loss - f64(ref)) ** 2))
    psc = np.sqrt(inten * in_) * mtch
    tot = psc.reshape(len(psc), -1, D).sum(axis=2)
    tl = tot[:, unstriped(lib)]
    norm = inten.reshape(len(inten), -1, D).sum(axis=2)
    nl2 = norm[:, unstriped(lib)]
    hid = f64(unit) * (tl - (0.6 * np.log(nl2)))
    return unpack_fp4(w3_words, w3_scales).T @ mxq(hid, 0, "e4m3")

@@ -1,0 +1,313 @@
+from contextlib import ExitStack
+
+import concourse.mybir as mybir
+from concourse.masks import make_identity
+
+K, T, S, D, N, H, V, U = 512, 2048, 1024, 4, 256, 512, 256, 512
+FLOPS = 2 * K * H * S * 2 + 2 * H * N * U
+
+F32 = mybir.dt.float32
+BF16 = mybir.dt.bfloat16
+I32 = mybir.dt.int32
+U32 = mybir.dt.uint32
+U16 = mybir.dt.uint16
+U8 = mybir.dt.uint8
+FP8X4 = mybir.dt.float8_e4m3fn_x4
+FP4X4 = mybir.dt.float4_e2m1fn_x4
+ACT = mybir.ActivationFunctionType
+ALU = mybir.AluOpType
+
+P = 128
+PACK = 4
+HALF = 512
+TINY = 2.0**-60
+LIB_PIECE = 128
+
+
+def tile_picked_ybioms_log_p_kernel(
+    tc, x_words, x_scales, w1_words, w1_scales, w2_words, w2_scales, ref, unit, w3_words, w3_scales, offs, nl, lib, out
+):
+    nc = tc.nc
+    with ExitStack() as ctx:
+        keep = ctx.enter_context(tc.tile_pool(name="keep", bufs=1))
+        psum = ctx.enter_context(tc.psum_pool(name="psum", bufs=1))
+
+        def bank(b, name):
+            return psum.tile([P, HALF], F32, name=name, tag="bank%d" % b)
+
+        def wide(name, tag=None):
+            return keep.tile([P, S], F32, name=name, tag=tag or name, align_bytes=64)
+
+        def load_scale_rows(plane, rows, queues):
+            for q in range(4):
+                queues[q].dma_start(plane[32 * q : 32 * q + 4, :].bitcast(I32), rows[0, 4 * q : 4 * q + 4, :].bitcast(I32))
+
+        offs_sb = keep.tile([P, S // 16], U16, name="offs_sb")
+        nl_sb = keep.tile([P, S // 16], U16, name="nl_sb")
+        lib_sb = keep.tile([P, U // 16], U16, name="lib_sb")
+
+        x_plane = keep.tile([P, T], U8, name="x_plane", align_bytes=64)
+        w_plane_raw = [keep.tile([P, H], U8, name="w_plane_raw%d" % i, align_bytes=64) for i in range(2)]
+        nc.gpsimd.memset(x_plane[:].bitcast(I32), 0)
+        for plane in reversed(w_plane_raw):
+            nc.gpsimd.memset(plane[:].bitcast(I32), 0)
+
+        nc.sync.dma_start(offs_sb[:], offs)
+        load_scale_rows(x_plane, x_scales, [nc.sync] * 4)
+        w_raw = [keep.tile([P, 2 * H], U8, name="w_raw%d" % i, tag="ref%d" % (2 - i), align_bytes=64) for i in range(2)]
+        nc.sync.dma_start(w_raw[1][:].bitcast(I32), w2_words[0].bitcast(I32))
+        x_table = keep.tile([P, T], I32, name="x_table", align_bytes=64)
+        nc.sync.dma_start(x_table[:], x_words[0].rearrange("p n t -> p (n t)").bitcast(I32))
+        nc.sync.dma_start(w_raw[0][:].bitcast(I32), w1_words[0].bitcast(I32))
+        load_scale_rows(w_plane_raw[1], w2_scales, [nc.sync] * 4)
+        load_scale_rows(w_plane_raw[0], w1_scales, [nc.sync] * 2 + [nc.gpsimd] * 2)
+        nc.sync.dma_start(nl_sb[:], nl)
+        tiny = keep.tile([P, 1], F32, name="tiny")
+        nc.gpsimd.memset(tiny[:], TINY)
+        ident = keep.tile([P, P], F32, name="ident", align_bytes=64)
+        make_identity(nc, ident[:])
+
+        x_codes = {}
+        x_bytes = [keep.tile([P, HALF], U8, name="x_bytes%d" % h, align_bytes=64) for h in range(2)]
+        w_codes = [keep.tile([P, 2 * H], U8, name="w_codes%d" % i, align_bytes=64) for i in range(2)]
+        w_bytes = [keep.tile([P, H], U8, name="w_bytes%d" % i, align_bytes=64) for i in range(2)]
+
+        def entries(lst, first, count):
+            return lst[:, first // 16 : (first + count) // 16]
+
+        def pick_bytes(h):
+            nc.vector.tensor_copy(x_bytes[h][:], x_plane[:].indirect(entries(offs_sb, h * HALF, HALF)))
+
+        def pick_words(h, tag):
+            x_codes[h] = keep.tile([P, HALF], U32, name="x_codes%d" % h, tag=tag, align_bytes=64)
+            nc.vector.tensor_copy(x_codes[h][:], x_table[:].bitcast(U32).indirect(entries(offs_sb, h * HALF, HALF)))
+
+        def deal(i):
+            nc.vector.tensor_copy(
+                w_codes[i][:].rearrange("p (t m b) -> p t m b", t=PACK, b=2),
+                w_raw[i][:].rearrange("p (m t b) -> p t m b", t=PACK, b=2),
+            )
+            nc.vector.tensor_copy(
+                w_bytes[i][:].rearrange("p (t m) -> p t m", t=PACK),
+                w_plane_raw[i][:].rearrange("p (m t) -> p t m", t=PACK),
+            )
+
+        pick_bytes(0)
+        pick_bytes(1)
+        pick_words(0, "x_codes0")
+        deal(1)
+        pick_words(1, "w_plane_raw1")
+        deal(0)
+
+        def product(i, t, h, acc):
+            nc.tensor.matmul_mx(
+                out=acc[:],
+                lhsT=w_codes[i][:, 2 * P * t : 2 * P * (t + 1)].bitcast(FP4X4),
+                lhsT_scale=w_bytes[i][:, P * t : P * (t + 1)],
+                rhs=x_codes[h][:].bitcast(FP8X4),
+                rhs_scale=x_bytes[h][:],
+                start=True,
+                stop=True,
+            )
+
+        def half(h):
+            return slice(h * HALF, (h + 1) * HALF)
+
+        mz_bank = [[0, 2], [1, 3], [4, 5], [6, 7]]
+        it_bank = [[0, 1], [2, 3], [4, 5], [6, 7]]
+        mass = [wide("mass%d" % t) for t in range(PACK)]
+        sig = [wide("sig%d" % t) for t in range(PACK)]
+        it_acc = {}
+
+        def masses(t, h):
+            acc = bank(mz_bank[t][h], "mz%d_%d" % (t, h))
+            product(1, t, h, acc)
+            nc.scalar.activation(mass[t][:, half(h)], acc[:], ACT.Sigmoid, scale=2.0)
+
+        def sigmoids(t, h):
+            acc = bank(it_bank[t][h], "it%d_%d" % (t, h))
+            product(0, t, h, acc)
+            nc.scalar.activation(sig[t][:, half(h)], acc[:], ACT.Sigmoid, scale=-1.0)
+            it_acc[t, h] = acc
+
+        ref_rows = ref.rearrange("(p t) j -> p t j", t=PACK)
+        miss = [wide("miss%d" % t) for t in range(PACK)]
+
+        def mismatch(t):
+            ref_sb = wide("ref_sb%d" % t, tag="ref%d" % (t % 3))
+            nc.sync.dma_start(ref_sb[:], ref_rows[:, t, :])
+            own = wide("own%d" % t, tag="own%d" % (t % 2))
+            nc.vector.scalar_tensor_tensor(own[:], ref_sb[:], -0.5, mass[t][:], ALU.mult, ALU.add)
+            for h in range(2):
+                nc.vector.tensor_tensor(
+                    miss[t][:, half(h)], mass[t][:].indirect(entries(nl_sb, h * HALF, HALF)), own[:, half(h)], ALU.subtract
+                )
+
+        for h in range(2):
+            masses(0, h)
+            masses(1, h)
+        mismatch(0)
+        for t in range(2, PACK):
+            for h in range(2):
+                masses(t, h)
+        mismatch(1)
+        for t in range(PACK):
+            for h in range(2):
+                sigmoids(t, h)
+        mismatch(2)
+
+        unit_sb = keep.tile([P, PACK], F32, name="unit_sb", tag="own0", align_bytes=64)
+        nc.sync.dma_start(unit_sb[:], unit.rearrange("(p t) o -> p (t o)", t=PACK))
+        nc.sync.dma_start(lib_sb[:], lib)
+        w3_codes = keep.tile([P, 2 * N], U8, name="w3_codes", tag="w_plane_raw1", align_bytes=64)
+        nc.sync.dma_start(w3_codes[:].bitcast(I32), w3_words[0].bitcast(I32))
+        w3_plane = keep.tile([P, N], U8, name="w3_plane", tag="w_plane_raw0", align_bytes=64)
+        nc.gpsimd.memset(w3_plane[:].bitcast(I32), 0)
+        load_scale_rows(w3_plane, w3_scales, [nc.sync] * 4)
+
+        neg_inten = [wide("neg_inten%d" % t) for t in range(PACK)]
+        log_inten = [wide("log_inten%d" % t) for t in range(PACK)]
+        log_norm_t = [keep.tile([P, V], F32, name="log_norm_t%d" % t, align_bytes=64) for t in range(PACK)]
+
+        def log_sigmoid(t):
+            nc.scalar.activation(sig[t][:], sig[t][:], ACT.Ln, bias=tiny[:])
+
+        def softplus(t):
+            for h in range(2):
+                nc.vector.scalar_tensor_tensor(
+                    neg_inten[t][:, half(h)], it_acc[t, h][:], -1.0, sig[t][:, half(h)], ALU.mult, ALU.min
+                )
+
+        def group_sums(acc, member, groups):
+            for g in groups:
+                for d in range(D):
+                    nc.tensor.matmul(
+                        acc[:, g * P : (g + 1) * P], member(g, d), ident[:], start=(d == 0), stop=(d == D - 1), is_transpose=True
+                    )
+
+        def logs(t):
+            nc.scalar.activation(log_inten[t][:], neg_inten[t][:], ACT.Ln, bias=tiny[:], scale=-1.0)
+
+        def norms(t):
+            acc = bank(t % 2, "norm%d" % t)
+            group_sums(acc, lambda g, d: neg_inten[t][:, g * HALF + d : (g + 1) * HALF : D], range(2))
+            nc.scalar.activation(log_norm_t[t][:], acc[:, :V], ACT.Ln, bias=tiny[:], scale=-1.0)
+
+        def square(t):
+            nc.scalar.activation(miss[t][:], miss[t][:], ACT.Square)
+
+        log_sigmoid(0)
+        softplus(0)
+        log_sigmoid(1)
+        softplus(1)
+        log_sigmoid(2)
+        log_sigmoid(3)
+        mismatch(3)
+        square(0)
+        logs(0)
+        logs(1)
+        norms(0)
+        square(1)
+        norms(1)
+        softplus(2)
+        softplus(3)
+        logs(2)
+        square(2)
+        logs(3)
+        norms(2)
+        square(3)
+        norms(3)
+
+        picked = [keep.tile([P, PACK, U // 2], BF16, name="picked%d" % r, align_bytes=64) for r in range(2)]
+        hid_v = [keep.tile([P, V], F32, name="hid_v%d" % t, align_bytes=64) for t in range(PACK)]
+        own_log, both, psc, tot_acc = {}, {}, {}, {}
+        last = PACK - 1
+
+        def own_part(t, tag):
+            own_log[t] = wide("own_log%d" % t, tag=tag)
+            nc.vector.scalar_tensor_tensor(own_log[t][:], miss[t][:], -12.0, log_inten[t][:], ALU.mult, ALU.add)
+
+        def partner_part(t, h, tag):
+            both[t, h] = keep.tile([P, HALF], F32, name="both%d_%d" % (t, h), tag=tag, align_bytes=64)
+            nc.vector.tensor_tensor(
+                both[t, h][:], log_inten[t][:].indirect(entries(nl_sb, h * HALF, HALF)), own_log[t][:, half(h)], ALU.add
+            )
+
+        def scores(t, h, tag, b):
+            psc[t, h] = keep.tile([P, D, P], F32, name="psc%d_%d" % (t, h), tag=tag, align_bytes=64)
+            nc.scalar.activation(
+                psc[t, h][:].rearrange("p d v -> p v d"), both[t, h][:].rearrange("p (v d) -> p v d", d=D), ACT.Exp, scale=0.5
+            )
+            if (t, b) not in tot_acc:
+                tot_acc[t, b] = bank(b, "tot%d_%d" % (t, h))
+            group_sums(tot_acc[t, b], lambda g, d: psc[t, g][:, d, :], [h])
+
+        def hidden(t, groups, b_in, b_out):
+            cols = slice(groups[0] * P, (groups[-1] + 1) * P)
+            mixed = keep.tile([P, V], F32, name="mixed%d_%d" % (t, groups[0]), align_bytes=64)
+            nc.vector.scalar_tensor_tensor(mixed[:, cols], log_norm_t[t][:, cols], -0.6, tot_acc[t, b_in][:, cols], ALU.mult, ALU.add)
+            back = bank(b_out, "back%d_%d" % (t, groups[0]))
+            for g in groups:
+                nc.tensor.transpose(back[:, g * P : (g + 1) * P], mixed[:, g * P : (g + 1) * P], ident[:])
+            nc.scalar.activation(hid_v[t][:, cols], back[:, cols], ACT.Copy, scale=unit_sb[:, t : t + 1])
+
+        def look_up(t, piece, on_vector):
+            r, c = divmod(piece * LIB_PIECE, U // 2)
+            dst = picked[r][:, t, c : c + LIB_PIECE]
+            src = hid_v[t][:].indirect(entries(lib_sb, piece * LIB_PIECE, LIB_PIECE))
+            if on_vector:
+                nc.vector.tensor_copy(dst, src)
+            else:
+                nc.scalar.activation(dst, src, ACT.Copy)
+
+        for t in range(last):
+            own_part(t, "sig%d" % t)
+            for h in range(2):
+                partner_part(t, h, "both%d_%d" % (t, h))
+        scores(0, 0, "neg_inten%d" % last, 2)
+        scores(0, 1, "both0_0", 2)
+        for t in range(1, last):
+            scores(t, 0, "both%d_1" % (t - 1), 2 + t)
+            scores(t, 1, "both%d_0" % t, 2 + t)
+        hidden(0, [0, 1], 2, 5)
+        own_part(last, "log_norm_t0")
+        hidden(1, [0, 1], 3, 6)
+        partner_part(last, 0, "log_norm_t1")
+        hidden(2, [0, 1], 4, 7)
+        partner_part(last, 1, "log_norm_t2")
+        for t in range(2):
+            for piece in range(U // LIB_PIECE):
+                look_up(t, piece, False)
+        scores(last, 0, "psc_last0", 2)
+        scores(last, 1, "psc_last1", 3)
+        for piece in range(U // LIB_PIECE):
+            look_up(2, piece, True)
+        hidden(last, [0], 2, 4)
+        hidden(last, [1], 3, 5)
+
+        for r in range(2):
+            look_up(PACK - 1, 2 * r, r == 0)
+            look_up(PACK - 1, 2 * r + 1, False)
+        for r in range(2):
+            grouped = keep.tile([P, U // 2, PACK], BF16, name="grouped%d" % r, align_bytes=64)
+            nc.vector.tensor_copy(grouped[:], picked[r][:].rearrange("p t r -> p r t"))
+            codes = keep.tile([P, U // 2], U32, name="codes%d" % r, align_bytes=64)
+            plane = keep.tile([P, U // 2], U8, name="plane%d" % r, align_bytes=64)
+            nc.vector.quantize_mx(out=codes[:].bitcast(FP8X4), scales=plane[:], in_=grouped[:].rearrange("p r t -> p (r t)"))
+            for m in range(N // P):
+                acc = bank([0, 1, 6, 7][2 * r + m], "out%d_%d" % (r, m))
+                nc.tensor.matmul_mx(
+                    out=acc[:, : U // 2],
+                    lhsT=w3_codes[:, 2 * P * m : 2 * P * (m + 1)].bitcast(FP4X4),
+                    lhsT_scale=w3_plane[:, P * m : P * (m + 1)],
+                    rhs=codes[:].bitcast(FP8X4),
+                    rhs_scale=plane[:],
+                    start=True,
+                    stop=True,
+                )
+                result = keep.tile([P, U // 2], F32, name="result%d_%d" % (r, m), align_bytes=64)
+                if r == 1 and m == 1:
+                    nc.vector.tensor_copy(result[:], acc[:, : U // 2])
+                else:
+                    nc.scalar.copy(result[:], acc[:, : U // 2])
+                nc.sync.dma_start(out[m * P : (m + 1) * P, r * (U // 2) : (r + 1) * (U // 2)], result[:])

@@ -1,7 +1,6 @@
 from contextlib import ExitStack
 
 import concourse.mybir as mybir
-from concourse.masks import make_identity
 
 K, T, S, D, N, H, V, U = 512, 2048, 1024, 4, 256, 512, 256, 512
 FLOPS = 2 * K * H * S * 2 + 2 * H * N * U
@@ -21,7 +20,6 @@ P = 128
 PACK = 4
 HALF = 512
 TINY = 2.0**-60
-LIB_PIECE = 128
 
 
 def tile_picked_ybioms_log_p_kernel(
@@ -30,6 +28,7 @@ def tile_picked_ybioms_log_p_kernel(
     nc = tc.nc
     with ExitStack() as ctx:
         keep = ctx.enter_context(tc.tile_pool(name="keep", bufs=1))
+        early_pool = ctx.enter_context(tc.tile_pool(name="early_pool", bufs=1))
         psum = ctx.enter_context(tc.psum_pool(name="psum", bufs=1))
 
         def bank(b, name):
@@ -38,38 +37,48 @@ def tile_picked_ybioms_log_p_kernel(
         def wide(name, tag=None):
             return keep.tile([P, S], F32, name=name, tag=tag or name, align_bytes=64)
 
-        def load_scale_rows(plane, rows, queues):
+        def load_scale_rows(plane, rows, queue):
             for q in range(4):
-                queues[q].dma_start(plane[32 * q : 32 * q + 4, :].bitcast(I32), rows[0, 4 * q : 4 * q + 4, :].bitcast(I32))
+                queue.dma_start(plane[32 * q : 32 * q + 4, :].bitcast(I32), rows[0, 4 * q : 4 * q + 4, :].bitcast(I32))
 
         offs_sb = keep.tile([P, S // 16], U16, name="offs_sb")
         nl_sb = keep.tile([P, S // 16], U16, name="nl_sb")
         lib_sb = keep.tile([P, U // 16], U16, name="lib_sb")
 
-        x_plane = keep.tile([P, T], U8, name="x_plane", align_bytes=64)
-        w_plane_raw = [keep.tile([P, H], U8, name="w_plane_raw%d" % i, align_bytes=64) for i in range(2)]
-        nc.gpsimd.memset(x_plane[:].bitcast(I32), 0)
-        for plane in reversed(w_plane_raw):
-            nc.gpsimd.memset(plane[:].bitcast(I32), 0)
-
-        nc.sync.dma_start(offs_sb[:], offs)
-        load_scale_rows(x_plane, x_scales, [nc.sync] * 4)
-        w_raw = [keep.tile([P, 2 * H], U8, name="w_raw%d" % i, tag="ref%d" % (2 - i), align_bytes=64) for i in range(2)]
-        nc.sync.dma_start(w_raw[1][:].bitcast(I32), w2_words[0].bitcast(I32))
-        x_table = keep.tile([P, T], I32, name="x_table", align_bytes=64)
-        nc.sync.dma_start(x_table[:], x_words[0].rearrange("p n t -> p (n t)").bitcast(I32))
-        nc.sync.dma_start(w_raw[0][:].bitcast(I32), w1_words[0].bitcast(I32))
-        load_scale_rows(w_plane_raw[1], w2_scales, [nc.sync] * 4)
-        load_scale_rows(w_plane_raw[0], w1_scales, [nc.sync] * 2 + [nc.gpsimd] * 2)
-        nc.sync.dma_start(nl_sb[:], nl)
+        x_plane = keep.tile([P, T], U8, name="x_plane", tag="ref0", align_bytes=64)
+        table_bytes = 4 * T
+        ones = early_pool.tile([P, 16], F32, name="ones", offset=table_bytes - 32)
         tiny = keep.tile([P, 1], F32, name="tiny")
-        nc.gpsimd.memset(tiny[:], TINY)
+        nc.vector.memset(x_plane[:].bitcast(I32), 0)
+        nc.vector.memset(ones[:, 0:1], 1.0)
+        nc.vector.tensor_scalar(tiny[:], ones[:, 0:1], TINY, None, ALU.mult)
+        w_raw = [keep.tile([P, 2 * H], U8, name="w_raw%d" % i, tag="ref%d" % (2 - i), align_bytes=64) for i in range(2)]
+        nc.gpsimd.dma_start(w_raw[1][:].bitcast(I32), w2_words[0].bitcast(I32))
+        nc.gpsimd.dma_start(w_raw[0][:].bitcast(I32), w1_words[0].bitcast(I32))
+        zeros = keep.tile([P, P], F32, name="zeros", tag="w1_plane_raw", align_bytes=64)
         ident = keep.tile([P, P], F32, name="ident", align_bytes=64)
-        make_identity(nc, ident[:])
+        nc.gpsimd.memset(zeros[:], 0.0)
+        nc.gpsimd.affine_select(
+            out=ident[:], in_=zeros[:], compare_op=ALU.not_equal, fill=1.0, base=0, pattern=[[-1, P]], channel_multiplier=1
+        )
+        x_table = early_pool.tile([P, T], I32, name="x_table", offset=0, align_bytes=64)
+        w_plane_raw = [
+            keep.tile([P, H], U8, name="w1_plane_raw", align_bytes=64),
+            early_pool.tile([P, H], U8, name="w2_plane_raw", offset=table_bytes, align_bytes=64),
+        ]
+        nc.sync.dma_start(offs_sb[:], offs)
+        load_scale_rows(x_plane, x_scales, nc.sync)
+        nc.sync.dma_start(x_table[:], x_words[0].rearrange("p n t -> p (n t)").bitcast(I32))
+        nc.sync.dma_start(nl_sb[:], nl)
+        nc.sync.dma_start(lib_sb[:], lib)
+        nc.vector.memset(w_plane_raw[1][:].bitcast(I32), 0)
+        load_scale_rows(w_plane_raw[1], w2_scales, nc.sync)
+        nc.gpsimd.memset(w_plane_raw[0][:].bitcast(I32), 0)
+        load_scale_rows(w_plane_raw[0], w1_scales, nc.sync)
 
         x_codes = {}
         x_bytes = [keep.tile([P, HALF], U8, name="x_bytes%d" % h, align_bytes=64) for h in range(2)]
-        w_codes = [keep.tile([P, 2 * H], U8, name="w_codes%d" % i, align_bytes=64) for i in range(2)]
+        w_codes = {}
         w_bytes = [keep.tile([P, H], U8, name="w_bytes%d" % i, align_bytes=64) for i in range(2)]
 
         def entries(lst, first, count):
@@ -82,22 +91,26 @@ def tile_picked_ybioms_log_p_kernel(
             x_codes[h] = keep.tile([P, HALF], U32, name="x_codes%d" % h, tag=tag, align_bytes=64)
             nc.vector.tensor_copy(x_codes[h][:], x_table[:].bitcast(U32).indirect(entries(offs_sb, h * HALF, HALF)))
 
-        def deal(i):
-            nc.vector.tensor_copy(
-                w_codes[i][:].rearrange("p (t m b) -> p t m b", t=PACK, b=2),
-                w_raw[i][:].rearrange("p (m t b) -> p t m b", t=PACK, b=2),
+        def deal(i, first, count):
+            tiles = slice(first, first + count)
+            nc.gpsimd.tensor_copy(
+                w_codes[i][:].rearrange("p (t m b) -> p t m b", t=PACK, b=2)[:, tiles],
+                w_raw[i][:].rearrange("p (m t b) -> p t m b", t=PACK, b=2)[:, tiles],
             )
-            nc.vector.tensor_copy(
-                w_bytes[i][:].rearrange("p (t m) -> p t m", t=PACK),
-                w_plane_raw[i][:].rearrange("p (m t) -> p t m", t=PACK),
+            nc.gpsimd.tensor_copy(
+                w_bytes[i][:].rearrange("p (t m) -> p t m", t=PACK)[:, tiles],
+                w_plane_raw[i][:].rearrange("p (m t) -> p t m", t=PACK)[:, tiles],
             )
 
+        w_codes[1] = keep.tile([P, 2 * H], U8, name="w_codes1", align_bytes=64)
+        deal(1, 0, 2)
+        deal(1, 2, 2)
+        w_codes[0] = early_pool.tile([P, 2 * H], U8, name="w_codes0", offset=table_bytes, align_bytes=64)
+        deal(0, 0, PACK)
         pick_bytes(0)
         pick_bytes(1)
         pick_words(0, "x_codes0")
-        deal(1)
-        pick_words(1, "w_plane_raw1")
-        deal(0)
+        pick_words(1, "x_codes1")
 
         def product(i, t, h, acc):
             nc.tensor.matmul_mx(
@@ -122,7 +135,10 @@ def tile_picked_ybioms_log_p_kernel(
         def masses(t, h):
             acc = bank(mz_bank[t][h], "mz%d_%d" % (t, h))
             product(1, t, h, acc)
-            nc.scalar.activation(mass[t][:, half(h)], acc[:], ACT.Sigmoid, scale=2.0)
+            if t == PACK - 1:
+                nc.scalar.activation(mass[t][:, half(h)], acc[:], ACT.Tanh)
+            else:
+                nc.scalar.activation(mass[t][:, half(h)], acc[:], ACT.Sigmoid, scale=2.0)
 
         def sigmoids(t, h):
             acc = bank(it_bank[t][h], "it%d_%d" % (t, h))
@@ -131,13 +147,20 @@ def tile_picked_ybioms_log_p_kernel(
             it_acc[t, h] = acc
 
         ref_rows = ref.rearrange("(p t) j -> p t j", t=PACK)
-        miss = [wide("miss%d" % t) for t in range(PACK)]
+        miss = {}
 
         def mismatch(t):
             ref_sb = wide("ref_sb%d" % t, tag="ref%d" % (t % 3))
             nc.sync.dma_start(ref_sb[:], ref_rows[:, t, :])
-            own = wide("own%d" % t, tag="own%d" % (t % 2))
-            nc.vector.scalar_tensor_tensor(own[:], ref_sb[:], -0.5, mass[t][:], ALU.mult, ALU.add)
+            if t == PACK - 1:
+                own = wide("own%d" % t, tag="own0")
+                nc.gpsimd.tensor_tensor(own[:], mass[t][:], ref_sb[:], ALU.subtract)
+                miss[t] = wide("miss%d" % t, tag="sig%d" % t)
+            else:
+                own = wide("own%d" % t, tag="own%d" % (t % 2))
+                for cols in [half(0), half(1)] if t < 2 else [slice(0, S)]:
+                    nc.vector.scalar_tensor_tensor(own[:, cols], ref_sb[:, cols], -0.5, mass[t][:, cols], ALU.mult, ALU.add)
+                miss[t] = wide("miss%d" % t)
             for h in range(2):
                 nc.vector.tensor_tensor(
                     miss[t][:, half(h)], mass[t][:].indirect(entries(nl_sb, h * HALF, HALF)), own[:, half(h)], ALU.subtract
@@ -156,14 +179,13 @@ def tile_picked_ybioms_log_p_kernel(
                 sigmoids(t, h)
         mismatch(2)
 
-        unit_sb = keep.tile([P, PACK], F32, name="unit_sb", tag="own0", align_bytes=64)
+        unit_sb = keep.tile([P, PACK], F32, name="unit_sb", tag="own1", align_bytes=64)
         nc.sync.dma_start(unit_sb[:], unit.rearrange("(p t) o -> p (t o)", t=PACK))
-        nc.sync.dma_start(lib_sb[:], lib)
-        w3_codes = keep.tile([P, 2 * N], U8, name="w3_codes", tag="w_plane_raw1", align_bytes=64)
+        w3_codes = keep.tile([P, 2 * N], U8, name="w3_codes", tag="x_bytes0", align_bytes=64)
         nc.sync.dma_start(w3_codes[:].bitcast(I32), w3_words[0].bitcast(I32))
-        w3_plane = keep.tile([P, N], U8, name="w3_plane", tag="w_plane_raw0", align_bytes=64)
-        nc.gpsimd.memset(w3_plane[:].bitcast(I32), 0)
-        load_scale_rows(w3_plane, w3_scales, [nc.sync] * 4)
+        w3_plane = keep.tile([P, N], U8, name="w3_plane", tag="x_bytes1", align_bytes=64)
+        nc.vector.memset(w3_plane[:].bitcast(I32), 0)
+        load_scale_rows(w3_plane, w3_scales, nc.sync)
 
         neg_inten = [wide("neg_inten%d" % t) for t in range(PACK)]
         log_inten = [wide("log_inten%d" % t) for t in range(PACK)]
@@ -189,49 +211,55 @@ def tile_picked_ybioms_log_p_kernel(
             nc.scalar.activation(log_inten[t][:], neg_inten[t][:], ACT.Ln, bias=tiny[:], scale=-1.0)
 
         def norms(t):
-            acc = bank(t % 2, "norm%d" % t)
+            acc = bank(2 * t, "norm%d" % t)
             group_sums(acc, lambda g, d: neg_inten[t][:, g * HALF + d : (g + 1) * HALF : D], range(2))
             nc.scalar.activation(log_norm_t[t][:], acc[:, :V], ACT.Ln, bias=tiny[:], scale=-1.0)
 
         def square(t):
             nc.scalar.activation(miss[t][:], miss[t][:], ACT.Square)
 
-        log_sigmoid(0)
-        softplus(0)
-        log_sigmoid(1)
-        softplus(1)
-        log_sigmoid(2)
-        log_sigmoid(3)
+        for t in range(PACK):
+            log_sigmoid(t)
+            softplus(t)
         mismatch(3)
         square(0)
         logs(0)
+        square(1)
         logs(1)
         norms(0)
-        square(1)
-        norms(1)
-        softplus(2)
-        softplus(3)
         logs(2)
+        norms(1)
         square(2)
         logs(3)
         norms(2)
-        square(3)
         norms(3)
 
-        picked = [keep.tile([P, PACK, U // 2], BF16, name="picked%d" % r, align_bytes=64) for r in range(2)]
-        hid_v = [keep.tile([P, V], F32, name="hid_v%d" % t, align_bytes=64) for t in range(PACK)]
+        picked = keep.tile([P, PACK * U], BF16, name="picked", align_bytes=64)
+        borrowed = picked[:, 2 * U : 3 * U].bitcast(F32)
+        hid_v = miss
         own_log, both, psc, tot_acc = {}, {}, {}, {}
         last = PACK - 1
 
         def own_part(t, tag):
             own_log[t] = wide("own_log%d" % t, tag=tag)
-            nc.vector.scalar_tensor_tensor(own_log[t][:], miss[t][:], -12.0, log_inten[t][:], ALU.mult, ALU.add)
+            nc.vector.scalar_tensor_tensor(own_log[t][:], miss[t][:], -3.0 if t == last else -12.0, log_inten[t][:], ALU.mult, ALU.add)
 
         def partner_part(t, h, tag):
             both[t, h] = keep.tile([P, HALF], F32, name="both%d_%d" % (t, h), tag=tag, align_bytes=64)
             nc.vector.tensor_tensor(
                 both[t, h][:], log_inten[t][:].indirect(entries(nl_sb, h * HALF, HALF)), own_log[t][:, half(h)], ALU.add
             )
+
+        def last_partner(first, count, dst):
+            nc.vector.tensor_tensor(
+                dst, log_inten[last][:].indirect(entries(nl_sb, first, count)), own_log[last][:, first : first + count], ALU.add
+            )
+
+        def last_scores(first, count, src, tag):
+            weighted = keep.tile([P, count], F32, name="weighted%d" % first, tag=tag, align_bytes=64)
+            nc.scalar.activation(weighted[:], src, ACT.Exp, scale=0.5)
+            groups = slice(first // D, (first + count) // D)
+            nc.vector.tensor_reduce(last_tot[:, groups], weighted[:].rearrange("p (v d) -> p v d", d=D), mybir.AxisListType.X, ALU.add)
 
         def scores(t, h, tag, b):
             psc[t, h] = keep.tile([P, D, P], F32, name="psc%d_%d" % (t, h), tag=tag, align_bytes=64)
@@ -244,58 +272,79 @@ def tile_picked_ybioms_log_p_kernel(
 
         def hidden(t, groups, b_in, b_out):
             cols = slice(groups[0] * P, (groups[-1] + 1) * P)
-            mixed = keep.tile([P, V], F32, name="mixed%d_%d" % (t, groups[0]), align_bytes=64)
+            mixed = borrowed if t == 2 else keep.tile([P, V], F32, name="mixed%d" % t, align_bytes=64)
             nc.vector.scalar_tensor_tensor(mixed[:, cols], log_norm_t[t][:, cols], -0.6, tot_acc[t, b_in][:, cols], ALU.mult, ALU.add)
             back = bank(b_out, "back%d_%d" % (t, groups[0]))
             for g in groups:
                 nc.tensor.transpose(back[:, g * P : (g + 1) * P], mixed[:, g * P : (g + 1) * P], ident[:])
             nc.scalar.activation(hid_v[t][:, cols], back[:, cols], ACT.Copy, scale=unit_sb[:, t : t + 1])
 
-        def look_up(t, piece, on_vector):
-            r, c = divmod(piece * LIB_PIECE, U // 2)
-            dst = picked[r][:, t, c : c + LIB_PIECE]
-            src = hid_v[t][:].indirect(entries(lib_sb, piece * LIB_PIECE, LIB_PIECE))
+        def look_up(t, first, count, on_vector):
+            dst = picked[:, t * U + first : t * U + first + count]
+            src = hid_v[t][:].indirect(entries(lib_sb, first, count))
             if on_vector:
                 nc.vector.tensor_copy(dst, src)
             else:
                 nc.scalar.activation(dst, src, ACT.Copy)
 
-        for t in range(last):
+        last_tot = keep.tile([P, V], F32, name="last_tot", align_bytes=64)
+        last_log = keep.tile([P, V], F32, name="last_log", align_bytes=64)
+        log_factor = keep.tile([P, 1], F32, name="log_factor")
+        nc.gpsimd.tensor_scalar(log_factor[:], unit_sb[:, last : last + 1], -0.6, 0.0, ALU.mult, ALU.add)
+        turned = bank(4, "turned")
+        for g in range(2):
+            nc.tensor.transpose(turned[:, g * P : (g + 1) * P], log_norm_t[last][:, g * P : (g + 1) * P], ident[:])
+        nc.vector.tensor_scalar(last_log[:], turned[:, :V], log_factor[:], None, ALU.mult)
+
+        def look_up_tile(t):
+            look_up(t, 0, U, False)
+
+        for t in range(2):
             own_part(t, "sig%d" % t)
             for h in range(2):
                 partner_part(t, h, "both%d_%d" % (t, h))
-        scores(0, 0, "neg_inten%d" % last, 2)
-        scores(0, 1, "both0_0", 2)
-        for t in range(1, last):
-            scores(t, 0, "both%d_1" % (t - 1), 2 + t)
-            scores(t, 1, "both%d_0" % t, 2 + t)
-        hidden(0, [0, 1], 2, 5)
-        own_part(last, "log_norm_t0")
-        hidden(1, [0, 1], 3, 6)
-        partner_part(last, 0, "log_norm_t1")
-        hidden(2, [0, 1], 4, 7)
-        partner_part(last, 1, "log_norm_t2")
-        for t in range(2):
-            for piece in range(U // LIB_PIECE):
-                look_up(t, piece, False)
-        scores(last, 0, "psc_last0", 2)
-        scores(last, 1, "psc_last1", 3)
-        for piece in range(U // LIB_PIECE):
-            look_up(2, piece, True)
-        hidden(last, [0], 2, 4)
-        hidden(last, [1], 3, 5)
+        scores(0, 0, "neg_inten%d" % last, 1)
+        scores(0, 1, "both0_0", 1)
+        square(last)
+        scores(1, 0, "both0_1", 3)
+        scores(1, 1, "both1_0", 3)
+        own_part(2, "sig2")
+        partner_part(2, 0, "both2_0")
+        hidden(0, [0, 1], 1, 7)
+        partner_part(2, 1, "log_norm_t0")
+        scores(2, 0, "both1_1", 5)
+        scores(2, 1, "both2_0", 5)
+        look_up_tile(0)
+        hidden(1, [0, 1], 3, 0)
+        own_part(last, "log_norm_t1")
+        look_up_tile(1)
+        hidden(2, [0, 1], 5, 2)
+        early = keep.tile([P, S - V], F32, name="early", tag="log_norm_t2", align_bytes=64)
+        pieces = [
+            (0, HALF, early[:, :HALF], "miss1"),
+            (HALF, V, early[:, HALF:], "weighted_mid"),
+            (S - V, V, borrowed, "weighted_last"),
+        ]
+        for first, count, piece, tag in pieces:
+            last_partner(first, count, piece)
+        for first, count, piece, tag in pieces:
+            last_scores(first, count, piece, tag)
+        look_up_tile(2)
+        nc.vector.scalar_tensor_tensor(hid_v[last][:, :V], last_tot[:], unit_sb[:, last : last + 1], last_log[:], ALU.mult, ALU.add)
 
         for r in range(2):
-            look_up(PACK - 1, 2 * r, r == 0)
-            look_up(PACK - 1, 2 * r + 1, False)
+            look_up(last, r * (U // 2), U // 2, r == 0)
         for r in range(2):
             grouped = keep.tile([P, U // 2, PACK], BF16, name="grouped%d" % r, align_bytes=64)
-            nc.vector.tensor_copy(grouped[:], picked[r][:].rearrange("p t r -> p r t"))
+            if r == 0:
+                nc.vector.tensor_copy(grouped[:], picked[:].rearrange("p (t r) -> p r t", t=PACK)[:, r * (U // 2) : (r + 1) * (U // 2), :])
+            else:
+                nc.scalar.copy(grouped[:], picked[:].rearrange("p (t r) -> p r t", t=PACK)[:, r * (U // 2) : (r + 1) * (U // 2), :])
             codes = keep.tile([P, U // 2], U32, name="codes%d" % r, align_bytes=64)
             plane = keep.tile([P, U // 2], U8, name="plane%d" % r, align_bytes=64)
             nc.vector.quantize_mx(out=codes[:].bitcast(FP8X4), scales=plane[:], in_=grouped[:].rearrange("p r t -> p (r t)"))
             for m in range(N // P):
-                acc = bank([0, 1, 6, 7][2 * r + m], "out%d_%d" % (r, m))
+                acc = bank(4 + 2 * r + m, "out%d_%d" % (r, m))
                 nc.tensor.matmul_mx(
                     out=acc[:, : U // 2],
                     lhsT=w3_codes[:, 2 * P * m : 2 * P * (m + 1)].bitcast(FP4X4),

@@ -1,3 +1,4 @@
+import math
 from contextlib import ExitStack
 
 import concourse.mybir as mybir
@@ -19,6 +20,7 @@ ALU = mybir.AluOpType
 P = 128
 PACK = 4
 HALF = 512
+ON_TENSOR = (0,)
 TINY = 2.0**-60
 
 
@@ -78,8 +80,7 @@ def tile_picked_ybioms_log_p_kernel(
 
         x_codes = {}
         x_bytes = [keep.tile([P, HALF], U8, name="x_bytes%d" % h, align_bytes=64) for h in range(2)]
-        w_codes = {}
-        w_bytes = [keep.tile([P, H], U8, name="w_bytes%d" % i, align_bytes=64) for i in range(2)]
+        w_codes, w_bytes = {}, {}
 
         def entries(lst, first, count):
             return lst[:, first // 16 : (first + count) // 16]
@@ -91,32 +92,40 @@ def tile_picked_ybioms_log_p_kernel(
             x_codes[h] = keep.tile([P, HALF], U32, name="x_codes%d" % h, tag=tag, align_bytes=64)
             nc.vector.tensor_copy(x_codes[h][:], x_table[:].bitcast(U32).indirect(entries(offs_sb, h * HALF, HALF)))
 
-        def deal(i, first, count):
-            tiles = slice(first, first + count)
-            nc.gpsimd.tensor_copy(
-                w_codes[i][:].rearrange("p (t m b) -> p t m b", t=PACK, b=2)[:, tiles],
-                w_raw[i][:].rearrange("p (m t b) -> p t m b", t=PACK, b=2)[:, tiles],
-            )
-            nc.gpsimd.tensor_copy(
-                w_bytes[i][:].rearrange("p (t m) -> p t m", t=PACK)[:, tiles],
-                w_plane_raw[i][:].rearrange("p (m t) -> p t m", t=PACK)[:, tiles],
+        def deal_words(engine, i, pair, dst):
+            w_codes[i, pair] = dst
+            engine.tensor_copy(
+                dst[:].rearrange("p (t m b) -> p t m b", t=2, b=2),
+                w_raw[i][:].rearrange("p (m t b) -> p t m b", t=PACK, b=2)[:, 2 * pair : 2 * pair + 2],
             )
 
-        w_codes[1] = keep.tile([P, 2 * H], U8, name="w_codes1", align_bytes=64)
-        deal(1, 0, 2)
-        deal(1, 2, 2)
-        w_codes[0] = early_pool.tile([P, 2 * H], U8, name="w_codes0", offset=table_bytes, align_bytes=64)
-        deal(0, 0, PACK)
+        def deal_bytes(engine, i, pair, dst):
+            w_bytes[i, pair] = dst
+            engine.tensor_copy(
+                dst[:].rearrange("p (t m) -> p t m", t=2),
+                w_plane_raw[i][:].rearrange("p (m t) -> p t m", t=PACK)[:, 2 * pair : 2 * pair + 2],
+            )
+
+        def placed(name, width, offset):
+            return early_pool.tile([P, width], U8, name=name, offset=offset, align_bytes=64)
+
+        for pair in range(2):
+            deal_words(nc.gpsimd, 1, pair, keep.tile([P, H], U8, name="w2_codes%d" % pair, align_bytes=64))
+            deal_bytes(nc.gpsimd, 1, pair, keep.tile([P, H // 2], U8, name="w2_bytes%d" % pair, align_bytes=64))
+        deal_words(nc.gpsimd, 0, 0, placed("w1_codes0", H, table_bytes))
         pick_bytes(0)
         pick_bytes(1)
         pick_words(0, "x_codes0")
         pick_words(1, "x_codes1")
+        deal_bytes(nc.vector, 0, 0, placed("w1_bytes0", H // 2, 0))
+        deal_bytes(nc.vector, 0, 1, placed("w1_bytes1", H // 2, H // 2))
+        deal_words(nc.vector, 0, 1, placed("w1_codes1", H, H))
 
         def product(i, t, h, acc):
             nc.tensor.matmul_mx(
                 out=acc[:],
-                lhsT=w_codes[i][:, 2 * P * t : 2 * P * (t + 1)].bitcast(FP4X4),
-                lhsT_scale=w_bytes[i][:, P * t : P * (t + 1)],
+                lhsT=w_codes[i, t // 2][:, 2 * P * (t % 2) : 2 * P * (t % 2 + 1)].bitcast(FP4X4),
+                lhsT_scale=w_bytes[i, t // 2][:, P * (t % 2) : P * (t % 2 + 1)],
                 rhs=x_codes[h][:].bitcast(FP8X4),
                 rhs_scale=x_bytes[h][:],
                 start=True,
@@ -158,7 +167,7 @@ def tile_picked_ybioms_log_p_kernel(
                 miss[t] = wide("miss%d" % t, tag="sig%d" % t)
             else:
                 own = wide("own%d" % t, tag="own%d" % (t % 2))
-                for cols in [half(0), half(1)] if t < 2 else [slice(0, S)]:
+                for cols in [half(0), half(1)] if t == 0 else [slice(0, S)]:
                     nc.vector.scalar_tensor_tensor(own[:, cols], ref_sb[:, cols], -0.5, mass[t][:, cols], ALU.mult, ALU.add)
                 miss[t] = wide("miss%d" % t)
             for h in range(2):
@@ -192,7 +201,8 @@ def tile_picked_ybioms_log_p_kernel(
         log_norm_t = [keep.tile([P, V], F32, name="log_norm_t%d" % t, align_bytes=64) for t in range(PACK)]
 
         def log_sigmoid(t):
-            nc.scalar.activation(sig[t][:], sig[t][:], ACT.Ln, bias=tiny[:])
+            for cols in [half(0), half(1)] if t == 0 else [slice(0, S)]:
+                nc.scalar.activation(sig[t][:, cols], sig[t][:, cols], ACT.Ln, bias=tiny[:])
 
         def softplus(t):
             for h in range(2):
@@ -216,12 +226,16 @@ def tile_picked_ybioms_log_p_kernel(
             nc.scalar.activation(log_norm_t[t][:], acc[:, :V], ACT.Ln, bias=tiny[:], scale=-1.0)
 
         def square(t):
-            nc.scalar.activation(miss[t][:], miss[t][:], ACT.Square)
+            nc.scalar.activation(miss[t][:], miss[t][:], ACT.Square, scale=math.sqrt(12.0) if t in ON_TENSOR else 1.0)
+
+        def square_beside(t):
+            nc.gpsimd.tensor_tensor(miss[t][:], miss[t][:], miss[t][:], ALU.mult)
 
         for t in range(PACK):
             log_sigmoid(t)
             softplus(t)
         mismatch(3)
+        square_beside(2)
         square(0)
         logs(0)
         square(1)
@@ -229,15 +243,15 @@ def tile_picked_ybioms_log_p_kernel(
         norms(0)
         logs(2)
         norms(1)
-        square(2)
         logs(3)
         norms(2)
         norms(3)
 
         picked = keep.tile([P, PACK * U], BF16, name="picked", align_bytes=64)
         borrowed = picked[:, 2 * U : 3 * U].bitcast(F32)
+        last_tot = keep.tile([P, V], F32, name="last_tot", align_bytes=64)
         hid_v = miss
-        own_log, both, psc, tot_acc = {}, {}, {}, {}
+        own_log, both, psc, tot_acc, expo = {}, {}, {}, {}, {}
         last = PACK - 1
 
         def own_part(t, tag):
@@ -250,6 +264,37 @@ def tile_picked_ybioms_log_p_kernel(
                 both[t, h][:], log_inten[t][:].indirect(entries(nl_sb, h * HALF, HALF)), own_log[t][:, half(h)], ALU.add
             )
 
+        def partner_minus_miss(t, h):
+            both[t, h] = keep.tile([P, HALF], F32, name="both%d_%d" % (t, h), align_bytes=64)
+            nc.vector.tensor_tensor(
+                both[t, h][:], log_inten[t][:].indirect(entries(nl_sb, h * HALF, HALF)), miss[t][:, half(h)], ALU.subtract
+            )
+            acc = bank(1 + 4 * t + 2 * h, "expo%d_%d" % (t, h))
+            for d in range(D):
+                cols = slice(d * P, (d + 1) * P)
+                nc.tensor.matmul(
+                    acc[:, cols], log_inten[t][:, h * HALF + d : (h + 1) * HALF : D], ident[:], start=True, stop=False, is_transpose=True
+                )
+                nc.tensor.matmul(acc[:, cols], both[t, h][:, d:HALF:D], ident[:], start=False, stop=True, is_transpose=True)
+            expo[t, h] = acc
+
+        def turned_scores(t, h, dst):
+            nc.scalar.activation(dst, expo[t, h][:], ACT.Exp, scale=0.5)
+            psc[t, h] = dst
+
+        def turned_hidden(t):
+            scaled = keep.tile([P, V], F32, name="scaled%d" % t, align_bytes=64)
+            nc.vector.tensor_scalar(scaled[:], log_norm_t[t][:], -0.6, None, ALU.mult)
+            back = bank(2 * t, "back%d" % t)
+            for g in range(2):
+                cols = slice(g * P, (g + 1) * P)
+                nc.tensor.matmul(back[:, cols], scaled[:, cols], ident[:], start=True, stop=False, is_transpose=True)
+                for d in range(D):
+                    nc.tensor.matmul(
+                        back[:, cols], psc[t, g][:, d * P : (d + 1) * P], ident[:], start=False, stop=(d == D - 1), is_transpose=True
+                    )
+            nc.scalar.activation(hid_v[t][:, :V], back[:, :V], ACT.Copy, scale=unit_sb[:, t : t + 1])
+
         def last_partner(first, count, dst):
             nc.vector.tensor_tensor(
                 dst, log_inten[last][:].indirect(entries(nl_sb, first, count)), own_log[last][:, first : first + count], ALU.add
@@ -260,11 +305,14 @@ def tile_picked_ybioms_log_p_kernel(
             nc.scalar.activation(weighted[:], src, ACT.Exp, scale=0.5)
             groups = slice(first // D, (first + count) // D)
             nc.vector.tensor_reduce(last_tot[:, groups], weighted[:].rearrange("p (v d) -> p v d", d=D), mybir.AxisListType.X, ALU.add)
+            nc.vector.scalar_tensor_tensor(
+                hid_v[last][:, groups], last_tot[:, groups], unit_sb[:, last : last + 1], last_log[:, groups], ALU.mult, ALU.add
+            )
 
-        def scores(t, h, tag, b):
-            psc[t, h] = keep.tile([P, D, P], F32, name="psc%d_%d" % (t, h), tag=tag, align_bytes=64)
+        def scores(t, h, dst, b):
+            psc[t, h] = dst.rearrange("p (d v) -> p d v", d=D)
             nc.scalar.activation(
-                psc[t, h][:].rearrange("p d v -> p v d"), both[t, h][:].rearrange("p (v d) -> p v d", d=D), ACT.Exp, scale=0.5
+                dst.rearrange("p (d v) -> p v d", d=D), both[t, h][:].rearrange("p (v d) -> p v d", d=D), ACT.Exp, scale=0.5
             )
             if (t, b) not in tot_acc:
                 tot_acc[t, b] = bank(b, "tot%d_%d" % (t, h))
@@ -287,59 +335,51 @@ def tile_picked_ybioms_log_p_kernel(
             else:
                 nc.scalar.activation(dst, src, ACT.Copy)
 
-        last_tot = keep.tile([P, V], F32, name="last_tot", align_bytes=64)
         last_log = keep.tile([P, V], F32, name="last_log", align_bytes=64)
         log_factor = keep.tile([P, 1], F32, name="log_factor")
         nc.gpsimd.tensor_scalar(log_factor[:], unit_sb[:, last : last + 1], -0.6, 0.0, ALU.mult, ALU.add)
-        turned = bank(4, "turned")
-        for g in range(2):
-            nc.tensor.transpose(turned[:, g * P : (g + 1) * P], log_norm_t[last][:, g * P : (g + 1) * P], ident[:])
-        nc.vector.tensor_scalar(last_log[:], turned[:, :V], log_factor[:], None, ALU.mult)
-
-        def look_up_tile(t):
-            look_up(t, 0, U, False)
-
-        for t in range(2):
+        for h in range(2):
+            partner_minus_miss(0, h)
+        for t in (1, 2):
             own_part(t, "sig%d" % t)
             for h in range(2):
                 partner_part(t, h, "both%d_%d" % (t, h))
-        scores(0, 0, "neg_inten%d" % last, 1)
-        scores(0, 1, "both0_0", 1)
+        early_scores = keep.tile([P, 3 * S], F32, name="early_scores", tag="neg_inten%d" % last, align_bytes=64)
+        for h in range(2):
+            turned_scores(0, h, early_scores[:, half(h)])
+            scores(1, h, early_scores[:, half(2 + h)], 5)
         square(last)
-        scores(1, 0, "both0_1", 3)
-        scores(1, 1, "both1_0", 3)
-        own_part(2, "sig2")
-        partner_part(2, 0, "both2_0")
-        hidden(0, [0, 1], 1, 7)
-        partner_part(2, 1, "log_norm_t0")
-        scores(2, 0, "both1_1", 5)
-        scores(2, 1, "both2_0", 5)
-        look_up_tile(0)
-        hidden(1, [0, 1], 3, 0)
+        turned_hidden(0)
+        for h in range(2):
+            scores(2, h, early_scores[:, half(4 + h)], 1)
+        turned = bank(4, "turned")
+        for g in range(2):
+            nc.tensor.transpose(turned[:, g * P : (g + 1) * P], log_norm_t[last][:, g * P : (g + 1) * P], ident[:])
+        nc.scalar.activation(last_log[:], turned[:, :V], ACT.Copy, scale=log_factor[:])
+        look_up(0, 0, U, False)
+        hidden(1, [0, 1], 5, 7)
+        look_up(1, 0, U, False)
         own_part(last, "log_norm_t1")
-        look_up_tile(1)
-        hidden(2, [0, 1], 5, 2)
-        early = keep.tile([P, S - V], F32, name="early", tag="log_norm_t2", align_bytes=64)
-        pieces = [
-            (0, HALF, early[:, :HALF], "miss1"),
-            (HALF, V, early[:, HALF:], "weighted_mid"),
-            (S - V, V, borrowed, "weighted_last"),
-        ]
-        for first, count, piece, tag in pieces:
-            last_partner(first, count, piece)
-        for first, count, piece, tag in pieces:
-            last_scores(first, count, piece, tag)
-        look_up_tile(2)
-        nc.vector.scalar_tensor_tensor(hid_v[last][:, :V], last_tot[:], unit_sb[:, last : last + 1], last_log[:], ALU.mult, ALU.add)
-
+        first_piece = keep.tile([P, HALF], F32, name="first_piece", align_bytes=64)
+        last_partner(0, HALF, first_piece[:])
+        hidden(2, [0, 1], 1, 3)
+        middle_piece = keep.tile([P, V], F32, name="middle_piece", tag="log_norm_t2", align_bytes=64)
+        last_partner(HALF, V, middle_piece[:])
+        last_partner(S - V, V, borrowed)
+        last_scores(0, HALF, first_piece[:], "miss1")
+        last_scores(HALF, V, middle_piece[:], "weighted_middle")
+        last_scores(S - V, V, borrowed, "weighted_last")
+        look_up(2, 0, U, False)
         for r in range(2):
             look_up(last, r * (U // 2), U // 2, r == 0)
         for r in range(2):
             grouped = keep.tile([P, U // 2, PACK], BF16, name="grouped%d" % r, align_bytes=64)
+            woven = grouped[:].rearrange("p (c i) t -> p c t i", i=4)
+            planes = picked[:].rearrange("p (t r c i) -> p r c t i", t=PACK, r=2, i=4)[:, r]
             if r == 0:
-                nc.vector.tensor_copy(grouped[:], picked[:].rearrange("p (t r) -> p r t", t=PACK)[:, r * (U // 2) : (r + 1) * (U // 2), :])
+                nc.vector.tensor_copy(woven, planes)
             else:
-                nc.scalar.copy(grouped[:], picked[:].rearrange("p (t r) -> p r t", t=PACK)[:, r * (U // 2) : (r + 1) * (U // 2), :])
+                nc.scalar.copy(woven, planes)
             codes = keep.tile([P, U // 2], U32, name="codes%d" % r, align_bytes=64)
             plane = keep.tile([P, U // 2], U8, name="plane%d" % r, align_bytes=64)
             nc.vector.quantize_mx(out=codes[:].bitcast(FP8X4), scales=plane[:], in_=grouped[:].rearrange("p r t -> p (r t)"))

@@ -54,7 +54,11 @@ def tile_picked_ybioms_log_p_kernel(
         nc.vector.memset(x_plane[:].bitcast(I32), 0)
         nc.vector.memset(ones[:, 0:1], 1.0)
         nc.vector.tensor_scalar(tiny[:], ones[:, 0:1], TINY, None, ALU.mult)
-        w_raw = [keep.tile([P, 2 * H], U8, name="w_raw%d" % i, tag="ref%d" % (2 - i), align_bytes=64) for i in range(2)]
+        words_at = table_bytes + 2 * H
+        w_raw = [
+            keep.tile([P, 2 * H], U8, name="w_raw0", tag="ref2", align_bytes=64),
+            early_pool.tile([P, 2 * H], U8, name="w_raw1", offset=words_at, align_bytes=64),
+        ]
         nc.gpsimd.dma_start(w_raw[1][:].bitcast(I32), w2_words[0].bitcast(I32))
         nc.gpsimd.dma_start(w_raw[0][:].bitcast(I32), w1_words[0].bitcast(I32))
         zeros = keep.tile([P, P], F32, name="zeros", tag="w1_plane_raw", align_bytes=64)
@@ -109,10 +113,11 @@ def tile_picked_ybioms_log_p_kernel(
         def placed(name, width, offset):
             return early_pool.tile([P, width], U8, name=name, offset=offset, align_bytes=64)
 
+        deal_words(nc.gpsimd, 1, 0, keep.tile([P, H], U8, name="w2_codes0", align_bytes=64))
         for pair in range(2):
-            deal_words(nc.gpsimd, 1, pair, keep.tile([P, H], U8, name="w2_codes%d" % pair, align_bytes=64))
             deal_bytes(nc.gpsimd, 1, pair, keep.tile([P, H // 2], U8, name="w2_bytes%d" % pair, align_bytes=64))
-        deal_words(nc.gpsimd, 0, 0, placed("w1_codes0", H, table_bytes))
+        deal_words(nc.gpsimd, 1, 1, placed("w2_codes1", H, table_bytes))
+        deal_words(nc.gpsimd, 0, 0, placed("w1_codes0", H, words_at - H + 64))
         pick_bytes(0)
         pick_bytes(1)
         pick_words(0, "x_codes0")
@@ -159,7 +164,10 @@ def tile_picked_ybioms_log_p_kernel(
         miss = {}
 
         def mismatch(t):
-            ref_sb = wide("ref_sb%d" % t, tag="ref%d" % (t % 3))
+            if t == 1:
+                ref_sb = early_pool.tile([P, S], F32, name="ref_sb1", offset=words_at + 64, align_bytes=64)
+            else:
+                ref_sb = wide("ref_sb%d" % t, tag="ref%d" % (t % 3))
             nc.sync.dma_start(ref_sb[:], ref_rows[:, t, :])
             if t == PACK - 1:
                 own = wide("own%d" % t, tag="own0")
@@ -305,6 +313,8 @@ def tile_picked_ybioms_log_p_kernel(
             nc.scalar.activation(weighted[:], src, ACT.Exp, scale=0.5)
             groups = slice(first // D, (first + count) // D)
             nc.vector.tensor_reduce(last_tot[:, groups], weighted[:].rearrange("p (v d) -> p v d", d=D), mybir.AxisListType.X, ALU.add)
+
+        def last_hidden(groups):
             nc.vector.scalar_tensor_tensor(
                 hid_v[last][:, groups], last_tot[:, groups], unit_sb[:, last : last + 1], last_log[:, groups], ALU.mult, ALU.add
             )
@@ -325,7 +335,10 @@ def tile_picked_ybioms_log_p_kernel(
             back = bank(b_out, "back%d_%d" % (t, groups[0]))
             for g in groups:
                 nc.tensor.transpose(back[:, g * P : (g + 1) * P], mixed[:, g * P : (g + 1) * P], ident[:])
-            nc.scalar.activation(hid_v[t][:, cols], back[:, cols], ACT.Copy, scale=unit_sb[:, t : t + 1])
+            if t == 2:
+                nc.vector.tensor_scalar(hid_v[t][:, cols], back[:, cols], unit_sb[:, t : t + 1], None, ALU.mult)
+            else:
+                nc.scalar.activation(hid_v[t][:, cols], back[:, cols], ACT.Copy, scale=unit_sb[:, t : t + 1])
 
         def look_up(t, first, count, on_vector):
             dst = picked[:, t * U + first : t * U + first + count]
@@ -358,7 +371,6 @@ def tile_picked_ybioms_log_p_kernel(
         nc.scalar.activation(last_log[:], turned[:, :V], ACT.Copy, scale=log_factor[:])
         look_up(0, 0, U, False)
         hidden(1, [0, 1], 5, 7)
-        look_up(1, 0, U, False)
         own_part(last, "log_norm_t1")
         first_piece = keep.tile([P, HALF], F32, name="first_piece", align_bytes=64)
         last_partner(0, HALF, first_piece[:])
@@ -366,27 +378,31 @@ def tile_picked_ybioms_log_p_kernel(
         middle_piece = keep.tile([P, V], F32, name="middle_piece", tag="log_norm_t2", align_bytes=64)
         last_partner(HALF, V, middle_piece[:])
         last_partner(S - V, V, borrowed)
-        last_scores(0, HALF, first_piece[:], "miss1")
-        last_scores(HALF, V, middle_piece[:], "weighted_middle")
+        last_scores(0, HALF, first_piece[:], "weighted_first")
+        look_up(1, 0, U, False)
+        last_scores(HALF, V, middle_piece[:], "miss1")
         last_scores(S - V, V, borrowed, "weighted_last")
+        last_hidden(slice(0, V))
         look_up(2, 0, U, False)
-        for r in range(2):
-            look_up(last, r * (U // 2), U // 2, r == 0)
-        for r in range(2):
-            grouped = keep.tile([P, U // 2, PACK], BF16, name="grouped%d" % r, align_bytes=64)
+        quarters = U // P
+        for r in range(quarters):
+            look_up(last, r * P, P, r == 0)
+        out_rows = out.rearrange("(m p) r -> p m r", p=P)
+        for r in range(quarters):
+            grouped = keep.tile([P, P, PACK], BF16, name="grouped%d" % r, align_bytes=64)
             woven = grouped[:].rearrange("p (c i) t -> p c t i", i=4)
-            planes = picked[:].rearrange("p (t r c i) -> p r c t i", t=PACK, r=2, i=4)[:, r]
-            if r == 0:
+            planes = picked[:].rearrange("p (t r c i) -> p r c t i", t=PACK, r=quarters, i=4)[:, r]
+            if r < 2:
                 nc.vector.tensor_copy(woven, planes)
             else:
                 nc.scalar.copy(woven, planes)
-            codes = keep.tile([P, U // 2], U32, name="codes%d" % r, align_bytes=64)
-            plane = keep.tile([P, U // 2], U8, name="plane%d" % r, align_bytes=64)
+            codes = keep.tile([P, P], U32, name="codes%d" % r, align_bytes=64)
+            plane = keep.tile([P, P], U8, name="plane%d" % r, align_bytes=64)
             nc.vector.quantize_mx(out=codes[:].bitcast(FP8X4), scales=plane[:], in_=grouped[:].rearrange("p r t -> p (r t)"))
+            acc = bank(4 + r, "out%d" % r)
             for m in range(N // P):
-                acc = bank(4 + 2 * r + m, "out%d_%d" % (r, m))
                 nc.tensor.matmul_mx(
-                    out=acc[:, : U // 2],
+                    out=acc[:, m * P : (m + 1) * P],
                     lhsT=w3_codes[:, 2 * P * m : 2 * P * (m + 1)].bitcast(FP4X4),
                     lhsT_scale=w3_plane[:, P * m : P * (m + 1)],
                     rhs=codes[:].bitcast(FP8X4),
@@ -394,9 +410,9 @@ def tile_picked_ybioms_log_p_kernel(
                     start=True,
                     stop=True,
                 )
-                result = keep.tile([P, U // 2], F32, name="result%d_%d" % (r, m), align_bytes=64)
-                if r == 1 and m == 1:
-                    nc.vector.tensor_copy(result[:], acc[:, : U // 2])
-                else:
-                    nc.scalar.copy(result[:], acc[:, : U // 2])
-                nc.sync.dma_start(out[m * P : (m + 1) * P, r * (U // 2) : (r + 1) * (U // 2)], result[:])
+            result = keep.tile([P, N], F32, name="result%d" % r, align_bytes=64)
+            if r == quarters - 1:
+                nc.vector.tensor_copy(result[:], acc[:, :N])
+            else:
+                nc.scalar.copy(result[:], acc[:, :N])
+            nc.sync.dma_start(out_rows[:, :, r * P : (r + 1) * P], result[:].rearrange("p (m r) -> p m r", r=P))

import math
from contextlib import ExitStack

import concourse.mybir as mybir

K, T, S, D, N, H, V, U = 512, 2048, 1024, 4, 256, 512, 256, 512
FLOPS = 2 * K * H * S * 2 + 2 * H * N * U

F32 = mybir.dt.float32
BF16 = mybir.dt.bfloat16
I32 = mybir.dt.int32
U32 = mybir.dt.uint32
U16 = mybir.dt.uint16
U8 = mybir.dt.uint8
FP8X4 = mybir.dt.float8_e4m3fn_x4
FP4X4 = mybir.dt.float4_e2m1fn_x4
ACT = mybir.ActivationFunctionType
ALU = mybir.AluOpType

P = 128
PACK = 4
HALF = 512
ON_TENSOR = (0,)
TINY = 2.0**-60


def tile_picked_ybioms_log_p_kernel(
    tc, x_words, x_scales, w1_words, w1_scales, w2_words, w2_scales, ref, unit, w3_words, w3_scales, offs, nl, lib, out
):
    nc = tc.nc
    with ExitStack() as ctx:
        keep = ctx.enter_context(tc.tile_pool(name="keep", bufs=1))
        early_pool = ctx.enter_context(tc.tile_pool(name="early_pool", bufs=1))
        psum = ctx.enter_context(tc.psum_pool(name="psum", bufs=1))

        def bank(b, name):
            return psum.tile([P, HALF], F32, name=name, tag="bank%d" % b)

        def wide(name, tag=None):
            return keep.tile([P, S], F32, name=name, tag=tag or name, align_bytes=64)

        def load_scale_rows(plane, rows, queue):
            for q in range(4):
                queue.dma_start(plane[32 * q : 32 * q + 4, :].bitcast(I32), rows[0, 4 * q : 4 * q + 4, :].bitcast(I32))

        offs_sb = keep.tile([P, S // 16], U16, name="offs_sb")
        nl_sb = keep.tile([P, S // 16], U16, name="nl_sb")
        lib_sb = keep.tile([P, U // 16], U16, name="lib_sb")

        x_plane = keep.tile([P, T], U8, name="x_plane", tag="ref0", align_bytes=64)
        table_bytes = 4 * T
        ones = early_pool.tile([P, 16], F32, name="ones", offset=table_bytes - 32)
        tiny = keep.tile([P, 1], F32, name="tiny")
        nc.vector.memset(x_plane[:].bitcast(I32), 0)
        nc.vector.memset(ones[:, 0:1], 1.0)
        nc.vector.tensor_scalar(tiny[:], ones[:, 0:1], TINY, None, ALU.mult)
        words_at = table_bytes + 2 * H
        w_raw = [
            keep.tile([P, 2 * H], U8, name="w_raw0", tag="ref2", align_bytes=64),
            early_pool.tile([P, 2 * H], U8, name="w_raw1", offset=words_at, align_bytes=64),
        ]
        nc.gpsimd.dma_start(w_raw[1][:].bitcast(I32), w2_words[0].bitcast(I32))
        nc.gpsimd.dma_start(w_raw[0][:].bitcast(I32), w1_words[0].bitcast(I32))
        zeros = keep.tile([P, P], F32, name="zeros", tag="w1_plane_raw", align_bytes=64)
        ident = keep.tile([P, P], F32, name="ident", align_bytes=64)
        nc.gpsimd.memset(zeros[:], 0.0)
        nc.gpsimd.affine_select(
            out=ident[:], in_=zeros[:], compare_op=ALU.not_equal, fill=1.0, base=0, pattern=[[-1, P]], channel_multiplier=1
        )
        x_table = early_pool.tile([P, T], I32, name="x_table", offset=0, align_bytes=64)
        w_plane_raw = [
            keep.tile([P, H], U8, name="w1_plane_raw", align_bytes=64),
            early_pool.tile([P, H], U8, name="w2_plane_raw", offset=table_bytes, align_bytes=64),
        ]
        nc.sync.dma_start(offs_sb[:], offs)
        load_scale_rows(x_plane, x_scales, nc.sync)
        nc.sync.dma_start(x_table[:], x_words[0].rearrange("p n t -> p (n t)").bitcast(I32))
        nc.sync.dma_start(nl_sb[:], nl)
        nc.sync.dma_start(lib_sb[:], lib)
        nc.vector.memset(w_plane_raw[1][:].bitcast(I32), 0)
        load_scale_rows(w_plane_raw[1], w2_scales, nc.sync)
        nc.gpsimd.memset(w_plane_raw[0][:].bitcast(I32), 0)
        load_scale_rows(w_plane_raw[0], w1_scales, nc.sync)

        x_codes = {}
        x_bytes = [keep.tile([P, HALF], U8, name="x_bytes%d" % h, align_bytes=64) for h in range(2)]
        w_codes, w_bytes = {}, {}

        def entries(lst, first, count):
            return lst[:, first // 16 : (first + count) // 16]

        def pick_bytes(h):
            nc.vector.tensor_copy(x_bytes[h][:], x_plane[:].indirect(entries(offs_sb, h * HALF, HALF)))

        def pick_words(h, tag):
            x_codes[h] = keep.tile([P, HALF], U32, name="x_codes%d" % h, tag=tag, align_bytes=64)
            nc.vector.tensor_copy(x_codes[h][:], x_table[:].bitcast(U32).indirect(entries(offs_sb, h * HALF, HALF)))

        def deal_words(engine, i, pair, dst):
            w_codes[i, pair] = dst
            engine.tensor_copy(
                dst[:].rearrange("p (t m b) -> p t m b", t=2, b=2),
                w_raw[i][:].rearrange("p (m t b) -> p t m b", t=PACK, b=2)[:, 2 * pair : 2 * pair + 2],
            )

        def deal_bytes(engine, i, pair, dst):
            w_bytes[i, pair] = dst
            engine.tensor_copy(
                dst[:].rearrange("p (t m) -> p t m", t=2),
                w_plane_raw[i][:].rearrange("p (m t) -> p t m", t=PACK)[:, 2 * pair : 2 * pair + 2],
            )

        def placed(name, width, offset):
            return early_pool.tile([P, width], U8, name=name, offset=offset, align_bytes=64)

        deal_words(nc.gpsimd, 1, 0, keep.tile([P, H], U8, name="w2_codes0", align_bytes=64))
        for pair in range(2):
            deal_bytes(nc.gpsimd, 1, pair, keep.tile([P, H // 2], U8, name="w2_bytes%d" % pair, align_bytes=64))
        deal_words(nc.gpsimd, 1, 1, placed("w2_codes1", H, table_bytes))
        deal_words(nc.gpsimd, 0, 0, placed("w1_codes0", H, words_at - H + 64))
        pick_bytes(0)
        pick_bytes(1)
        pick_words(0, "x_codes0")
        pick_words(1, "x_codes1")
        deal_bytes(nc.vector, 0, 0, placed("w1_bytes0", H // 2, 0))
        deal_bytes(nc.vector, 0, 1, placed("w1_bytes1", H // 2, H // 2))
        deal_words(nc.vector, 0, 1, placed("w1_codes1", H, H))

        def product(i, t, h, acc):
            nc.tensor.matmul_mx(
                out=acc[:],
                lhsT=w_codes[i, t // 2][:, 2 * P * (t % 2) : 2 * P * (t % 2 + 1)].bitcast(FP4X4),
                lhsT_scale=w_bytes[i, t // 2][:, P * (t % 2) : P * (t % 2 + 1)],
                rhs=x_codes[h][:].bitcast(FP8X4),
                rhs_scale=x_bytes[h][:],
                start=True,
                stop=True,
            )

        def half(h):
            return slice(h * HALF, (h + 1) * HALF)

        mz_bank = [[0, 2], [1, 3], [4, 5], [6, 7]]
        it_bank = [[0, 1], [2, 3], [4, 5], [6, 7]]
        mass = [wide("mass%d" % t) for t in range(PACK)]
        sig = [wide("sig%d" % t) for t in range(PACK)]
        it_acc = {}

        def masses(t, h):
            acc = bank(mz_bank[t][h], "mz%d_%d" % (t, h))
            product(1, t, h, acc)
            if t == PACK - 1:
                nc.scalar.activation(mass[t][:, half(h)], acc[:], ACT.Tanh)
            else:
                nc.scalar.activation(mass[t][:, half(h)], acc[:], ACT.Sigmoid, scale=2.0)

        def sigmoids(t, h):
            acc = bank(it_bank[t][h], "it%d_%d" % (t, h))
            product(0, t, h, acc)
            nc.scalar.activation(sig[t][:, half(h)], acc[:], ACT.Sigmoid, scale=-1.0)
            it_acc[t, h] = acc

        ref_rows = ref.rearrange("(p t) j -> p t j", t=PACK)
        miss = {}

        def mismatch(t):
            if t == 1:
                ref_sb = early_pool.tile([P, S], F32, name="ref_sb1", offset=words_at + 64, align_bytes=64)
            else:
                ref_sb = wide("ref_sb%d" % t, tag="ref%d" % (t % 3))
            nc.sync.dma_start(ref_sb[:], ref_rows[:, t, :])
            if t == PACK - 1:
                own = wide("own%d" % t, tag="own0")
                nc.gpsimd.tensor_tensor(own[:], mass[t][:], ref_sb[:], ALU.subtract)
                miss[t] = wide("miss%d" % t, tag="sig%d" % t)
            else:
                own = wide("own%d" % t, tag="own%d" % (t % 2))
                for cols in [half(0), half(1)] if t == 0 else [slice(0, S)]:
                    nc.vector.scalar_tensor_tensor(own[:, cols], ref_sb[:, cols], -0.5, mass[t][:, cols], ALU.mult, ALU.add)
                miss[t] = wide("miss%d" % t)
            for h in range(2):
                nc.vector.tensor_tensor(
                    miss[t][:, half(h)], mass[t][:].indirect(entries(nl_sb, h * HALF, HALF)), own[:, half(h)], ALU.subtract
                )

        for h in range(2):
            masses(0, h)
            masses(1, h)
        mismatch(0)
        for t in range(2, PACK):
            for h in range(2):
                masses(t, h)
        mismatch(1)
        for t in range(PACK):
            for h in range(2):
                sigmoids(t, h)
        mismatch(2)

        unit_sb = keep.tile([P, PACK], F32, name="unit_sb", tag="own1", align_bytes=64)
        nc.sync.dma_start(unit_sb[:], unit.rearrange("(p t) o -> p (t o)", t=PACK))
        w3_codes = keep.tile([P, 2 * N], U8, name="w3_codes", tag="x_bytes0", align_bytes=64)
        nc.sync.dma_start(w3_codes[:].bitcast(I32), w3_words[0].bitcast(I32))
        w3_plane = keep.tile([P, N], U8, name="w3_plane", tag="x_bytes1", align_bytes=64)
        nc.vector.memset(w3_plane[:].bitcast(I32), 0)
        load_scale_rows(w3_plane, w3_scales, nc.sync)

        neg_inten = [wide("neg_inten%d" % t) for t in range(PACK)]
        log_inten = [wide("log_inten%d" % t) for t in range(PACK)]
        log_norm_t = [keep.tile([P, V], F32, name="log_norm_t%d" % t, align_bytes=64) for t in range(PACK)]

        def log_sigmoid(t):
            for cols in [half(0), half(1)] if t == 0 else [slice(0, S)]:
                nc.scalar.activation(sig[t][:, cols], sig[t][:, cols], ACT.Ln, bias=tiny[:])

        def softplus(t):
            for h in range(2):
                nc.vector.scalar_tensor_tensor(
                    neg_inten[t][:, half(h)], it_acc[t, h][:], -1.0, sig[t][:, half(h)], ALU.mult, ALU.min
                )

        def group_sums(acc, member, groups):
            for g in groups:
                for d in range(D):
                    nc.tensor.matmul(
                        acc[:, g * P : (g + 1) * P], member(g, d), ident[:], start=(d == 0), stop=(d == D - 1), is_transpose=True
                    )

        def logs(t):
            nc.scalar.activation(log_inten[t][:], neg_inten[t][:], ACT.Ln, bias=tiny[:], scale=-1.0)

        def norms(t):
            acc = bank(2 * t, "norm%d" % t)
            group_sums(acc, lambda g, d: neg_inten[t][:, g * HALF + d : (g + 1) * HALF : D], range(2))
            nc.scalar.activation(log_norm_t[t][:], acc[:, :V], ACT.Ln, bias=tiny[:], scale=-1.0)

        def square(t):
            nc.scalar.activation(miss[t][:], miss[t][:], ACT.Square, scale=math.sqrt(12.0) if t in ON_TENSOR else 1.0)

        def square_beside(t):
            nc.gpsimd.tensor_tensor(miss[t][:], miss[t][:], miss[t][:], ALU.mult)

        for t in range(PACK):
            log_sigmoid(t)
            softplus(t)
        mismatch(3)
        square_beside(2)
        square(0)
        logs(0)
        square(1)
        logs(1)
        norms(0)
        logs(2)
        norms(1)
        logs(3)
        norms(2)
        norms(3)

        picked = keep.tile([P, PACK * U], BF16, name="picked", align_bytes=64)
        borrowed = picked[:, 2 * U : 3 * U].bitcast(F32)
        last_tot = keep.tile([P, V], F32, name="last_tot", align_bytes=64)
        hid_v = miss
        own_log, both, psc, tot_acc, expo = {}, {}, {}, {}, {}
        last = PACK - 1

        def own_part(t, tag):
            own_log[t] = wide("own_log%d" % t, tag=tag)
            nc.vector.scalar_tensor_tensor(own_log[t][:], miss[t][:], -3.0 if t == last else -12.0, log_inten[t][:], ALU.mult, ALU.add)

        def partner_part(t, h, tag):
            both[t, h] = keep.tile([P, HALF], F32, name="both%d_%d" % (t, h), tag=tag, align_bytes=64)
            nc.vector.tensor_tensor(
                both[t, h][:], log_inten[t][:].indirect(entries(nl_sb, h * HALF, HALF)), own_log[t][:, half(h)], ALU.add
            )

        def partner_minus_miss(t, h):
            both[t, h] = keep.tile([P, HALF], F32, name="both%d_%d" % (t, h), align_bytes=64)
            nc.vector.tensor_tensor(
                both[t, h][:], log_inten[t][:].indirect(entries(nl_sb, h * HALF, HALF)), miss[t][:, half(h)], ALU.subtract
            )
            acc = bank(1 + 4 * t + 2 * h, "expo%d_%d" % (t, h))
            for d in range(D):
                cols = slice(d * P, (d + 1) * P)
                nc.tensor.matmul(
                    acc[:, cols], log_inten[t][:, h * HALF + d : (h + 1) * HALF : D], ident[:], start=True, stop=False, is_transpose=True
                )
                nc.tensor.matmul(acc[:, cols], both[t, h][:, d:HALF:D], ident[:], start=False, stop=True, is_transpose=True)
            expo[t, h] = acc

        def turned_scores(t, h, dst):
            nc.scalar.activation(dst, expo[t, h][:], ACT.Exp, scale=0.5)
            psc[t, h] = dst

        def turned_hidden(t):
            scaled = keep.tile([P, V], F32, name="scaled%d" % t, align_bytes=64)
            nc.vector.tensor_scalar(scaled[:], log_norm_t[t][:], -0.6, None, ALU.mult)
            back = bank(2 * t, "back%d" % t)
            for g in range(2):
                cols = slice(g * P, (g + 1) * P)
                nc.tensor.matmul(back[:, cols], scaled[:, cols], ident[:], start=True, stop=False, is_transpose=True)
                for d in range(D):
                    nc.tensor.matmul(
                        back[:, cols], psc[t, g][:, d * P : (d + 1) * P], ident[:], start=False, stop=(d == D - 1), is_transpose=True
                    )
            nc.scalar.activation(hid_v[t][:, :V], back[:, :V], ACT.Copy, scale=unit_sb[:, t : t + 1])

        def last_partner(first, count, dst):
            nc.vector.tensor_tensor(
                dst, log_inten[last][:].indirect(entries(nl_sb, first, count)), own_log[last][:, first : first + count], ALU.add
            )

        def last_scores(first, count, src, tag):
            weighted = keep.tile([P, count], F32, name="weighted%d" % first, tag=tag, align_bytes=64)
            nc.scalar.activation(weighted[:], src, ACT.Exp, scale=0.5)
            groups = slice(first // D, (first + count) // D)
            nc.vector.tensor_reduce(last_tot[:, groups], weighted[:].rearrange("p (v d) -> p v d", d=D), mybir.AxisListType.X, ALU.add)

        def last_hidden(groups):
            nc.vector.scalar_tensor_tensor(
                hid_v[last][:, groups], last_tot[:, groups], unit_sb[:, last : last + 1], last_log[:, groups], ALU.mult, ALU.add
            )

        def scores(t, h, dst, b):
            psc[t, h] = dst.rearrange("p (d v) -> p d v", d=D)
            nc.scalar.activation(
                dst.rearrange("p (d v) -> p v d", d=D), both[t, h][:].rearrange("p (v d) -> p v d", d=D), ACT.Exp, scale=0.5
            )
            if (t, b) not in tot_acc:
                tot_acc[t, b] = bank(b, "tot%d_%d" % (t, h))
            group_sums(tot_acc[t, b], lambda g, d: psc[t, g][:, d, :], [h])

        def hidden(t, groups, b_in, b_out):
            cols = slice(groups[0] * P, (groups[-1] + 1) * P)
            mixed = borrowed if t == 2 else keep.tile([P, V], F32, name="mixed%d" % t, align_bytes=64)
            nc.vector.scalar_tensor_tensor(mixed[:, cols], log_norm_t[t][:, cols], -0.6, tot_acc[t, b_in][:, cols], ALU.mult, ALU.add)
            back = bank(b_out, "back%d_%d" % (t, groups[0]))
            for g in groups:
                nc.tensor.transpose(back[:, g * P : (g + 1) * P], mixed[:, g * P : (g + 1) * P], ident[:])
            if t == 2:
                nc.vector.tensor_scalar(hid_v[t][:, cols], back[:, cols], unit_sb[:, t : t + 1], None, ALU.mult)
            else:
                nc.scalar.activation(hid_v[t][:, cols], back[:, cols], ACT.Copy, scale=unit_sb[:, t : t + 1])

        def look_up(t, first, count, on_vector):
            dst = picked[:, t * U + first : t * U + first + count]
            src = hid_v[t][:].indirect(entries(lib_sb, first, count))
            if on_vector:
                nc.vector.tensor_copy(dst, src)
            else:
                nc.scalar.activation(dst, src, ACT.Copy)

        last_log = keep.tile([P, V], F32, name="last_log", align_bytes=64)
        log_factor = keep.tile([P, 1], F32, name="log_factor")
        nc.gpsimd.tensor_scalar(log_factor[:], unit_sb[:, last : last + 1], -0.6, 0.0, ALU.mult, ALU.add)
        for h in range(2):
            partner_minus_miss(0, h)
        for t in (1, 2):
            own_part(t, "sig%d" % t)
            for h in range(2):
                partner_part(t, h, "both%d_%d" % (t, h))
        early_scores = keep.tile([P, 3 * S], F32, name="early_scores", tag="neg_inten%d" % last, align_bytes=64)
        for h in range(2):
            turned_scores(0, h, early_scores[:, half(h)])
            scores(1, h, early_scores[:, half(2 + h)], 5)
        square(last)
        turned_hidden(0)
        for h in range(2):
            scores(2, h, early_scores[:, half(4 + h)], 1)
        turned = bank(4, "turned")
        for g in range(2):
            nc.tensor.transpose(turned[:, g * P : (g + 1) * P], log_norm_t[last][:, g * P : (g + 1) * P], ident[:])
        nc.scalar.activation(last_log[:], turned[:, :V], ACT.Copy, scale=log_factor[:])
        look_up(0, 0, U, False)
        hidden(1, [0, 1], 5, 7)
        own_part(last, "log_norm_t1")
        first_piece = keep.tile([P, HALF], F32, name="first_piece", align_bytes=64)
        last_partner(0, HALF, first_piece[:])
        hidden(2, [0, 1], 1, 3)
        middle_piece = keep.tile([P, V], F32, name="middle_piece", tag="log_norm_t2", align_bytes=64)
        last_partner(HALF, V, middle_piece[:])
        last_partner(S - V, V, borrowed)
        last_scores(0, HALF, first_piece[:], "weighted_first")
        look_up(1, 0, U, False)
        last_scores(HALF, V, middle_piece[:], "miss1")
        last_scores(S - V, V, borrowed, "weighted_last")
        last_hidden(slice(0, V))
        look_up(2, 0, U, False)
        quarters = U // P
        for r in range(quarters):
            look_up(last, r * P, P, r == 0)
        out_rows = out.rearrange("(m p) r -> p m r", p=P)
        for r in range(quarters):
            grouped = keep.tile([P, P, PACK], BF16, name="grouped%d" % r, align_bytes=64)
            woven = grouped[:].rearrange("p (c i) t -> p c t i", i=4)
            planes = picked[:].rearrange("p (t r c i) -> p r c t i", t=PACK, r=quarters, i=4)[:, r]
            if r < 2:
                nc.vector.tensor_copy(woven, planes)
            else:
                nc.scalar.copy(woven, planes)
            codes = keep.tile([P, P], U32, name="codes%d" % r, align_bytes=64)
            plane = keep.tile([P, P], U8, name="plane%d" % r, align_bytes=64)
            nc.vector.quantize_mx(out=codes[:].bitcast(FP8X4), scales=plane[:], in_=grouped[:].rearrange("p r t -> p (r t)"))
            acc = bank(4 + r, "out%d" % r)
            for m in range(N // P):
                nc.tensor.matmul_mx(
                    out=acc[:, m * P : (m + 1) * P],
                    lhsT=w3_codes[:, 2 * P * m : 2 * P * (m + 1)].bitcast(FP4X4),
                    lhsT_scale=w3_plane[:, P * m : P * (m + 1)],
                    rhs=codes[:].bitcast(FP8X4),
                    rhs_scale=plane[:],
                    start=True,
                    stop=True,
                )
            result = keep.tile([P, N], F32, name="result%d" % r, align_bytes=64)
            if r == quarters - 1:
                nc.vector.tensor_copy(result[:], acc[:, :N])
            else:
                nc.scalar.copy(result[:], acc[:, :N])
            nc.sync.dma_start(out_rows[:, :, r * P : (r + 1) * P], result[:].rearrange("p (m r) -> p m r", r=P))
